import numpy as np
import ml_dtypes


def mxq(x, axis, fmt="e4m3"):
    dtype, down = {"e4m3": (ml_dtypes.float8_e4m3fn, 7), "e5m2": (ml_dtypes.float8_e5m2, 14)}[fmt]
    v = np.moveaxis(np.asarray(x, np.float32).astype(ml_dtypes.bfloat16).astype(np.float64), axis, -1)
    blocks = v.reshape(v.shape[:-1] + (-1, 32))
    amax = np.abs(blocks).max(-1, keepdims=True)
    byte = np.maximum(np.where(amax > 0, np.frexp(amax)[1] - 1 + 127, 0) - down, 1)
    scale = np.exp2(byte - 127.0)
    codes = (blocks / scale).astype(np.float32).astype(dtype).astype(np.float64)
    return np.moveaxis((codes * scale).reshape(v.shape), -1, axis)


WIDE = False


def mx_kscale(k):
    if not WIDE:
        return np.ones(k)
    levels = np.array([10, -10, 5, -5, 0])
    if k % 512:
        return np.exp2(np.random.permutation(np.resize(levels, k // 32))).repeat(32)
    a = np.empty((k // 512, 16))
    for p in range(k // 512):
        a[p, :8] = np.random.permutation(np.resize(levels, 8))
        for g in range(8):
            far = levels[np.abs(levels - a[p, g]) >= 10]
            a[p, g + 8] = far[np.random.randint(len(far))]
    return np.exp2(a.ravel()).repeat(32)


def f64(x):
    return np.asarray(x).astype(np.float64)


def striped(idx):
    return np.tile(idx.reshape(-1, 16).T, (8, 1)).astype(np.uint16)


def unstriped(offs):
    return offs[:16].T.reshape(-1).astype(np.int64)


def pack_weight(w):
    k, n = w.shape
    w = f64(np.asarray(w, np.float32).astype(ml_dtypes.bfloat16)).reshape(k // 32, 32, n)
    amax = np.abs(w).max(1)
    byte = np.clip(np.where(amax > 0, np.frexp(amax)[1] - 1 + 127 - 7, 1), 1, 254)
    scaled = (w * np.exp2(127.0 - byte)[:, None, :]).reshape(k, n).astype(np.float32)
    words = np.ascontiguousarray(scaled.reshape(k // 512, 128, 4, n).transpose(0, 1, 3, 2)).astype(ml_dtypes.float8_e4m3fn).view(np.uint8)
    return words, np.ascontiguousarray(byte.astype(np.uint8).reshape(k // 512, 16, n))


def unpack_weight(words, scales):
    g, p, n, _ = words.shape
    vals = np.ascontiguousarray(words).view(ml_dtypes.float8_e4m3fn).astype(np.float64) * np.repeat(np.exp2(scales.astype(np.float64) - 127.0), 8, axis=1)[..., None]
    return vals.transpose(0, 1, 3, 2).reshape(g * 512, n)


def relu2(v):
    return np.maximum(v, 0.0) ** 2


K, T, D, S, V, N = 2048, 1024, 4, 1024, 256, 128


def setup_inputs():
    n = np.random.standard_normal
    s = mx_kscale(K)[:, None]
    packed = pack_weight(n((K, T)) * s)
    return {
        "x_words": packed[0],
        "x_scales": packed[1],
        "w": (n((D, K, N)) / np.sqrt(D * K) / s[None]).astype(np.float32),
        "b": (0.3 * n((N, 1))).astype(np.float32),
        "gate": np.tile(np.random.uniform(0.2, 1.0, S), (N, 1)).astype(np.float32),
        "offs": striped(np.random.permutation(T)[:S]),
    }


def reference(x_words, x_scales, w, b, gate, offs):
    idx = unstriped(offs)
    xq = unpack_weight(x_words, x_scales)[:, idx]
    wq = mxq(f64(w), 1, "e4m3")
    y = sum(wq[d].T @ xq[:, d * V:(d + 1) * V] for d in range(D))
    y = relu2(y + f64(b))
    out = np.zeros((N, T))
    out[:, idx] = f64(gate) * np.tile(y, (1, D))
    return out

@@ -1,0 +1,152 @@
+from contextlib import ExitStack
+
+import concourse.mybir as mybir
+
+K, T, D, V, M = 2048, 1024, 4, 256, 128
+FLOPS = 2 * D * K * M * V
+
+F32 = mybir.dt.float32
+BF16 = mybir.dt.bfloat16
+I32 = mybir.dt.int32
+U32 = mybir.dt.uint32
+U16 = mybir.dt.uint16
+U8 = mybir.dt.uint8
+FP8X4 = mybir.dt.float8_e4m3fn_x4
+ACT = mybir.ActivationFunctionType
+MULT = mybir.AluOpType.mult
+
+P = 128
+PACK = 4
+PASSES = K // (P * PACK)
+H = V // 2
+EARLY = T - H
+WORD_WINDOW = 1216
+BYTE_WINDOW = 1408
+
+
+def tile_picked_tome_lin_relu2_sub_p_kernel(tc, x_words, x_scales, w, b, gate, offs, out):
+    nc = tc.nc
+    with ExitStack() as ctx:
+        keep = ctx.enter_context(tc.tile_pool(name="keep", bufs=1))
+        psum = ctx.enter_context(tc.psum_pool(name="psum", bufs=1))
+
+        offsets = keep.tile([P, T // 16], U16, name="offsets")
+        nc.sync.dma_start(offsets[:], offs)
+
+        def entries(first, count):
+            return offsets[:, first // 16 : (first + count) // 16]
+
+        byte_table = keep.tile([P, BYTE_WINDOW], U8, name="byte_table", align_bytes=64)
+        nc.vector.memset(byte_table[:].bitcast(I32), 0)
+        for q in range(4):
+            nc.sync.dma_start(
+                byte_table[32 * q : 32 * q + 16, 0:T].bitcast(I32),
+                x_scales[:, 4 * q : 4 * q + 4, :].bitcast(I32),
+            )
+        word_table = keep.tile([P, (PASSES - 1) * T + WORD_WINDOW], I32, name="word_table", align_bytes=64)
+        nc.vector.memset(word_table[:, PASSES * T :], 0)
+
+        picked_bytes = keep.tile([P, T], U8, name="picked_bytes", align_bytes=64)
+        nc.vector.tensor_copy(picked_bytes[:], byte_table[:].indirect(offsets[:]))
+
+        acc = [psum.tile([P, H], F32, name="acc%d" % h) for h in range(2)]
+        picked_words = {}
+        codes = {}
+        planes = {}
+        started = set()
+
+        def load_tokens(o):
+            first = (PASSES - 1 - o) * T
+            nc.sync.dma_start(
+                word_table[:, first : first + T],
+                x_words[o].rearrange("p n t -> p (n t)").bitcast(I32),
+            )
+            early = keep.tile([P, EARLY], U32, name="early%d" % o, align_bytes=64)
+            nc.vector.tensor_copy(
+                early[:], word_table[:, first : first + WORD_WINDOW].bitcast(U32).indirect(entries(0, EARLY))
+            )
+            picked_words[o] = early
+
+        def multiply(o, d, h, words, last):
+            first = d * V + h * H
+            nc.tensor.matmul_mx(
+                out=acc[h][:],
+                lhsT=codes[o, d].bitcast(FP8X4),
+                lhsT_scale=planes[o, d],
+                rhs=words.bitcast(FP8X4),
+                rhs_scale=picked_bytes[PACK * o :, first : first + H],
+                start=(h not in started),
+                stop=last,
+            )
+            started.add(h)
+
+        def load_weights(o, d0, count, tag):
+            raw = keep.tile([P, count, PACK, M], F32, name="raw%d_%d" % (o, d0))
+            nc.sync.dma_start(
+                raw[:].rearrange("p d t m -> p d (t m)"),
+                w[d0 : d0 + count, o * P * PACK : (o + 1) * P * PACK, :].rearrange("d (p t) m -> p d (t m)", t=PACK),
+            )
+            rounded = keep.tile([P, count * M * PACK], BF16, name="rounded%d_%d" % (o, d0), tag=tag, align_bytes=64)
+            for j in range(count):
+                nc.scalar.copy(
+                    rounded[:, j * M * PACK : (j + 1) * M * PACK].rearrange("p (c i t) -> p c t i", i=4, t=PACK),
+                    raw[:, j].rearrange("p t (c i) -> p c t i", i=4),
+                )
+            w_codes = keep.tile([P, count * M], U32, name="w_codes%d_%d" % (o, d0), align_bytes=64)
+            w_plane = keep.tile([P, count * M], U8, name="w_plane%d_%d" % (o, d0), align_bytes=64)
+            nc.vector.quantize_mx(out=w_codes[:].bitcast(FP8X4), scales=w_plane[:], in_=rounded[:])
+            for j in range(count):
+                d = d0 + j
+                codes[o, d] = w_codes[:, j * M : (j + 1) * M]
+                planes[o, d] = w_plane[:, j * M : (j + 1) * M]
+
+        def multiply_early(o, d):
+            for h in range(2):
+                first = d * V + h * H
+                if first < EARLY:
+                    multiply(o, d, h, picked_words[o][:, first : first + H], h == 0 and (o, d) == (PASSES - 1, D - 1))
+
+        steps = [(0,), (0, 0, 2), (1,), (0, 2, 2), (2,), (1, 0, 2), (3,), (1, 2, 2), (2, 0, 2), (2, 2, 2), (3, 0, 2), (3, 2, 1), (3, 3, 1)]
+        done = set()
+        for step in steps:
+            if len(step) == 1:
+                load_tokens(step[0])
+            else:
+                o, d0, count = step
+                load_weights(o, d0, count, "last" if step == steps[-1] else "r%d_%d" % (o, d0))
+            for o in range(PASSES):
+                for d in range(D):
+                    if o in picked_words and (o, d) in codes and (o, d) not in done:
+                        done.add((o, d))
+                        multiply_early(o, d)
+
+        bias = keep.tile([P, 1], F32, name="bias")
+        nc.sync.dma_start(bias[:], b)
+        gates = keep.tile([P, T], F32, name="gates")
+        nc.sync.dma_start(gates[:], gate)
+
+        late = keep.tile([P, PASSES * H], U32, name="late", tag="last", align_bytes=64)
+        for o in range(PASSES):
+            first = (PASSES - 1 - o) * T
+            nc.vector.tensor_copy(
+                late[:, o * H : (o + 1) * H], word_table[:, first : first + T].bitcast(U32).indirect(entries(EARLY, H))
+            )
+            multiply(o, D - 1, 1, late[:, o * H : (o + 1) * H], o == PASSES - 1)
+
+        results = keep.tile([P, T], F32, name="results")
+        for h in range(2):
+            positive = keep.tile([P, H], F32, name="positive%d" % h)
+            nc.scalar.activation(positive[:], acc[h][:], ACT.Relu, bias=bias[:])
+            for d in ((0, 2, 1, 3) if h == 0 else (0, 1, 2, 3)):
+                first = d * V + h * H
+                nc.scalar.activation(results[:, first : first + H], positive[:], ACT.Square)
+
+        placed = keep.tile([P, T], F32, name="placed")
+        for first, count in ((0, H), (2 * V, H), (H, 3 * H), (2 * V + H, 3 * H)):
+            nc.vector.tensor_tensor(
+                placed[:].indirect(entries(first, count)),
+                results[:, first : first + count],
+                gates[:, first : first + count],
+                MULT,
+            )
+        nc.sync.dma_start(out, placed[:])

@@ -106,7 +106,7 @@ def tile_picked_tome_lin_relu2_sub_p_kernel(tc, x_words, x_scales, w, b, gate, o
                 if first < EARLY:
                     multiply(o, d, h, picked_words[o][:, first : first + H], h == 0 and (o, d) == (PASSES - 1, D - 1))
 
-        steps = [(0,), (0, 0, 2), (1,), (0, 2, 2), (2,), (1, 0, 2), (3,), (1, 2, 2), (2, 0, 2), (2, 2, 2), (3, 0, 2), (3, 2, 1), (3, 3, 1)]
+        steps = [(0,), (0, 0, 2), (0, 2, 2), (1,), (1, 0, 2), (1, 2, 2), (2,), (2, 0, 2), (2, 2, 2), (3,), (3, 0, 2), (3, 2, 1), (3, 3, 1)]
         done = set()
         for step in steps:
             if len(step) == 1:
@@ -137,12 +137,14 @@ def tile_picked_tome_lin_relu2_sub_p_kernel(tc, x_words, x_scales, w, b, gate, o
         for h in range(2):
             positive = keep.tile([P, H], F32, name="positive%d" % h)
             nc.scalar.activation(positive[:], acc[h][:], ACT.Relu, bias=bias[:])
-            for d in ((0, 2, 1, 3) if h == 0 else (0, 1, 2, 3)):
-                first = d * V + h * H
-                nc.scalar.activation(results[:, first : first + H], positive[:], ACT.Square)
+            slots = results[:].rearrange("p (d h v) -> p d h v", d=D, h=2)
+            for d0, d1 in (((0, 1), (1, 4)) if h == 0 else ((0, 2), (2, 4))):
+                nc.scalar.activation(
+                    slots[:, d0:d1, h, :], positive[:].unsqueeze(1).to_broadcast([P, d1 - d0, H]), ACT.Square
+                )
 
         placed = keep.tile([P, T], F32, name="placed")
-        for first, count in ((0, H), (2 * V, H), (H, 3 * H), (2 * V + H, 3 * H)):
+        for first, count in ((0, H), (H, 4 * H), (5 * H, 3 * H)):
             nc.vector.tensor_tensor(
                 placed[:].indirect(entries(first, count)),
                 results[:, first : first + count],

@@ -30,6 +30,16 @@ def tile_picked_tome_lin_relu2_sub_p_kernel(tc, x_words, x_scales, w, b, gate, o
         keep = ctx.enter_context(tc.tile_pool(name="keep", bufs=1))
         psum = ctx.enter_context(tc.psum_pool(name="psum", bufs=1))
 
+        word_table = keep.tile([P, (PASSES - 1) * T + WORD_WINDOW], I32, name="word_table", align_bytes=64)
+
+        def load_words(o):
+            first = (PASSES - 1 - o) * T
+            nc.sync.dma_start(
+                word_table[:, first : first + T],
+                x_words[o].rearrange("p n t -> p (n t)").bitcast(I32),
+            )
+
+        load_words(0)
         offsets = keep.tile([P, T // 16], U16, name="offsets")
         nc.sync.dma_start(offsets[:], offs)
 
@@ -43,7 +53,6 @@ def tile_picked_tome_lin_relu2_sub_p_kernel(tc, x_words, x_scales, w, b, gate, o
                 byte_table[32 * q : 32 * q + 16, 0:T].bitcast(I32),
                 x_scales[:, 4 * q : 4 * q + 4, :].bitcast(I32),
             )
-        word_table = keep.tile([P, (PASSES - 1) * T + WORD_WINDOW], I32, name="word_table", align_bytes=64)
         nc.vector.memset(word_table[:, PASSES * T :], 0)
 
         picked_bytes = keep.tile([P, T], U8, name="picked_bytes", align_bytes=64)
@@ -57,10 +66,8 @@ def tile_picked_tome_lin_relu2_sub_p_kernel(tc, x_words, x_scales, w, b, gate, o
 
         def load_tokens(o):
             first = (PASSES - 1 - o) * T
-            nc.sync.dma_start(
-                word_table[:, first : first + T],
-                x_words[o].rearrange("p n t -> p (n t)").bitcast(I32),
-            )
+            if o > 0:
+                load_words(o)
             early = keep.tile([P, EARLY], U32, name="early%d" % o, align_bytes=64)
             nc.vector.tensor_copy(
                 early[:], word_table[:, first : first + WORD_WINDOW].bitcast(U32).indirect(entries(0, EARLY))
@@ -87,11 +94,10 @@ def tile_picked_tome_lin_relu2_sub_p_kernel(tc, x_words, x_scales, w, b, gate, o
                 w[d0 : d0 + count, o * P * PACK : (o + 1) * P * PACK, :].rearrange("d (p t) m -> p d (t m)", t=PACK),
             )
             rounded = keep.tile([P, count * M * PACK], BF16, name="rounded%d_%d" % (o, d0), tag=tag, align_bytes=64)
-            for j in range(count):
-                nc.scalar.copy(
-                    rounded[:, j * M * PACK : (j + 1) * M * PACK].rearrange("p (c i t) -> p c t i", i=4, t=PACK),
-                    raw[:, j].rearrange("p t (c i) -> p c t i", i=4),
-                )
+            nc.scalar.copy(
+                rounded[:].rearrange("p (d c i t) -> p d c t i", d=count, i=2, t=PACK),
+                raw[:].rearrange("p d t (c i) -> p d c t i", i=2),
+            )
             w_codes = keep.tile([P, count * M], U32, name="w_codes%d_%d" % (o, d0), align_bytes=64)
             w_plane = keep.tile([P, count * M], U8, name="w_plane%d_%d" % (o, d0), align_bytes=64)
             nc.vector.quantize_mx(out=w_codes[:].bitcast(FP8X4), scales=w_plane[:], in_=rounded[:])
@@ -144,7 +150,7 @@ def tile_picked_tome_lin_relu2_sub_p_kernel(tc, x_words, x_scales, w, b, gate, o
                 )
 
         placed = keep.tile([P, T], F32, name="placed")
-        for first, count in ((0, H), (H, 4 * H), (5 * H, 3 * H)):
+        for first, count in ((0, H), (2 * V, H), (H, 3 * H), (2 * V + H, 3 * H)):
             nc.vector.tensor_tensor(
                 placed[:].indirect(entries(first, count)),
                 results[:, first : first + count],

@@ -20,7 +20,8 @@ PACK = 4
 PASSES = K // (P * PACK)
 H = V // 2
 EARLY = T - H
-WORD_WINDOW = 1216
+WORD_WINDOW = 1408
+WHOLE = 2
 BYTE_WINDOW = 1408
 
 
@@ -68,9 +69,10 @@ def tile_picked_tome_lin_relu2_sub_p_kernel(tc, x_words, x_scales, w, b, gate, o
             first = (PASSES - 1 - o) * T
             if o > 0:
                 load_words(o)
-            early = keep.tile([P, EARLY], U32, name="early%d" % o, align_bytes=64)
+            count = T if o < WHOLE else EARLY
+            early = keep.tile([P, count], U32, name="early%d" % o, align_bytes=64)
             nc.vector.tensor_copy(
-                early[:], word_table[:, first : first + WORD_WINDOW].bitcast(U32).indirect(entries(0, EARLY))
+                early[:], word_table[:, first : first + WORD_WINDOW].bitcast(U32).indirect(entries(0, count))
             )
             picked_words[o] = early
 
@@ -109,10 +111,10 @@ def tile_picked_tome_lin_relu2_sub_p_kernel(tc, x_words, x_scales, w, b, gate, o
         def multiply_early(o, d):
             for h in range(2):
                 first = d * V + h * H
-                if first < EARLY:
+                if first < EARLY or o < WHOLE:
                     multiply(o, d, h, picked_words[o][:, first : first + H], h == 0 and (o, d) == (PASSES - 1, D - 1))
 
-        steps = [(0,), (0, 0, 2), (0, 2, 2), (1,), (1, 0, 2), (1, 2, 2), (2,), (2, 0, 2), (2, 2, 2), (3,), (3, 0, 2), (3, 2, 1), (3, 3, 1)]
+        steps = [(0,), (0, 0, 4), (1,), (1, 0, 4), (2,), (2, 0, 2), (2, 2, 2), (3,), (3, 0, 1), (3, 1, 1), (3, 2, 1), (3, 3, 1)]
         done = set()
         for step in steps:
             if len(step) == 1:
@@ -131,18 +133,22 @@ def tile_picked_tome_lin_relu2_sub_p_kernel(tc, x_words, x_scales, w, b, gate, o
         gates = keep.tile([P, T], F32, name="gates")
         nc.sync.dma_start(gates[:], gate)
 
-        late = keep.tile([P, PASSES * H], U32, name="late", tag="last", align_bytes=64)
-        for o in range(PASSES):
+        late = keep.tile([P, (PASSES - WHOLE) * H], U32, name="late", tag="last", align_bytes=64)
+        for o in range(WHOLE, PASSES):
             first = (PASSES - 1 - o) * T
+            slot = (o - WHOLE) * H
             nc.vector.tensor_copy(
-                late[:, o * H : (o + 1) * H], word_table[:, first : first + T].bitcast(U32).indirect(entries(EARLY, H))
+                late[:, slot : slot + H], word_table[:, first : first + T].bitcast(U32).indirect(entries(EARLY, H))
             )
-            multiply(o, D - 1, 1, late[:, o * H : (o + 1) * H], o == PASSES - 1)
+            multiply(o, D - 1, 1, late[:, slot : slot + H], o == PASSES - 1)
 
         results = keep.tile([P, T], F32, name="results")
         for h in range(2):
             positive = keep.tile([P, H], F32, name="positive%d" % h)
-            nc.scalar.activation(positive[:], acc[h][:], ACT.Relu, bias=bias[:])
+            if h == 0:
+                nc.scalar.activation(positive[:], acc[h][:], ACT.Relu, bias=bias[:])
+            else:
+                nc.vector.tensor_scalar(positive[:], acc[h][:], bias[:], 0.0, mybir.AluOpType.add, mybir.AluOpType.max)
             slots = results[:].rearrange("p (d h v) -> p d h v", d=D, h=2)
             for d0, d1 in (((0, 1), (1, 4)) if h == 0 else ((0, 2), (2, 4))):
                 nc.scalar.activation(
@@ -150,7 +156,7 @@ def tile_picked_tome_lin_relu2_sub_p_kernel(tc, x_words, x_scales, w, b, gate, o
                 )
 
         placed = keep.tile([P, T], F32, name="placed")
-        for first, count in ((0, H), (2 * V, H), (H, 3 * H), (2 * V + H, 3 * H)):
+        for first, count in ((0, H), (H, 4 * H), (5 * H, 3 * H)):
             nc.vector.tensor_tensor(
                 placed[:].indirect(entries(first, count)),
                 results[:, first : first + count],

from contextlib import ExitStack

import concourse.mybir as mybir

K, T, D, V, M = 2048, 1024, 4, 256, 128
FLOPS = 2 * D * K * M * V

F32 = mybir.dt.float32
BF16 = mybir.dt.bfloat16
I32 = mybir.dt.int32
U32 = mybir.dt.uint32
U16 = mybir.dt.uint16
U8 = mybir.dt.uint8
FP8X4 = mybir.dt.float8_e4m3fn_x4
ACT = mybir.ActivationFunctionType
MULT = mybir.AluOpType.mult

P = 128
PACK = 4
PASSES = K // (P * PACK)
H = V // 2
EARLY = T - H
WORD_WINDOW = 1408
WHOLE = 2
BYTE_WINDOW = 1408


def tile_picked_tome_lin_relu2_sub_p_kernel(tc, x_words, x_scales, w, b, gate, offs, out):
    nc = tc.nc
    with ExitStack() as ctx:
        keep = ctx.enter_context(tc.tile_pool(name="keep", bufs=1))
        psum = ctx.enter_context(tc.psum_pool(name="psum", bufs=1))

        word_table = keep.tile([P, (PASSES - 1) * T + WORD_WINDOW], I32, name="word_table", align_bytes=64)

        def load_words(o):
            first = (PASSES - 1 - o) * T
            nc.sync.dma_start(
                word_table[:, first : first + T],
                x_words[o].rearrange("p n t -> p (n t)").bitcast(I32),
            )

        load_words(0)
        offsets = keep.tile([P, T // 16], U16, name="offsets")
        nc.sync.dma_start(offsets[:], offs)

        def entries(first, count):
            return offsets[:, first // 16 : (first + count) // 16]

        byte_table = keep.tile([P, BYTE_WINDOW], U8, name="byte_table", align_bytes=64)
        nc.vector.memset(byte_table[:].bitcast(I32), 0)
        for q in range(4):
            nc.sync.dma_start(
                byte_table[32 * q : 32 * q + 16, 0:T].bitcast(I32),
                x_scales[:, 4 * q : 4 * q + 4, :].bitcast(I32),
            )
        nc.vector.memset(word_table[:, PASSES * T :], 0)

        picked_bytes = keep.tile([P, T], U8, name="picked_bytes", align_bytes=64)
        nc.vector.tensor_copy(picked_bytes[:], byte_table[:].indirect(offsets[:]))

        acc = [psum.tile([P, H], F32, name="acc%d" % h) for h in range(2)]
        picked_words = {}
        codes = {}
        planes = {}
        started = set()

        def load_tokens(o):
            first = (PASSES - 1 - o) * T
            if o > 0:
                load_words(o)
            count = T if o < WHOLE else EARLY
            early = keep.tile([P, count], U32, name="early%d" % o, align_bytes=64)
            nc.vector.tensor_copy(
                early[:], word_table[:, first : first + WORD_WINDOW].bitcast(U32).indirect(entries(0, count))
            )
            picked_words[o] = early

        def multiply(o, d, h, words, last):
            first = d * V + h * H
            nc.tensor.matmul_mx(
                out=acc[h][:],
                lhsT=codes[o, d].bitcast(FP8X4),
                lhsT_scale=planes[o, d],
                rhs=words.bitcast(FP8X4),
                rhs_scale=picked_bytes[PACK * o :, first : first + H],
                start=(h not in started),
                stop=last,
            )
            started.add(h)

        def load_weights(o, d0, count, tag):
            raw = keep.tile([P, count, PACK, M], F32, name="raw%d_%d" % (o, d0))
            nc.sync.dma_start(
                raw[:].rearrange("p d t m -> p d (t m)"),
                w[d0 : d0 + count, o * P * PACK : (o + 1) * P * PACK, :].rearrange("d (p t) m -> p d (t m)", t=PACK),
            )
            rounded = keep.tile([P, count * M * PACK], BF16, name="rounded%d_%d" % (o, d0), tag=tag, align_bytes=64)
            nc.scalar.copy(
                rounded[:].rearrange("p (d c i t) -> p d c t i", d=count, i=2, t=PACK),
                raw[:].rearrange("p d t (c i) -> p d c t i", i=2),
            )
            w_codes = keep.tile([P, count * M], U32, name="w_codes%d_%d" % (o, d0), align_bytes=64)
            w_plane = keep.tile([P, count * M], U8, name="w_plane%d_%d" % (o, d0), align_bytes=64)
            nc.vector.quantize_mx(out=w_codes[:].bitcast(FP8X4), scales=w_plane[:], in_=rounded[:])
            for j in range(count):
                d = d0 + j
                codes[o, d] = w_codes[:, j * M : (j + 1) * M]
                planes[o, d] = w_plane[:, j * M : (j + 1) * M]

        def multiply_early(o, d):
            for h in range(2):
                first = d * V + h * H
                if first < EARLY or o < WHOLE:
                    multiply(o, d, h, picked_words[o][:, first : first + H], h == 0 and (o, d) == (PASSES - 1, D - 1))

        steps = [(0,), (0, 0, 4), (1,), (1, 0, 4), (2,), (2, 0, 2), (2, 2, 2), (3,), (3, 0, 1), (3, 1, 1), (3, 2, 1), (3, 3, 1)]
        done = set()
        for step in steps:
            if len(step) == 1:
                load_tokens(step[0])
            else:
                o, d0, count = step
                load_weights(o, d0, count, "last" if step == steps[-1] else "r%d_%d" % (o, d0))
            for o in range(PASSES):
                for d in range(D):
                    if o in picked_words and (o, d) in codes and (o, d) not in done:
                        done.add((o, d))
                        multiply_early(o, d)

        bias = keep.tile([P, 1], F32, name="bias")
        nc.sync.dma_start(bias[:], b)
        gates = keep.tile([P, T], F32, name="gates")
        nc.sync.dma_start(gates[:], gate)

        late = keep.tile([P, (PASSES - WHOLE) * H], U32, name="late", tag="last", align_bytes=64)
        for o in range(WHOLE, PASSES):
            first = (PASSES - 1 - o) * T
            slot = (o - WHOLE) * H
            nc.vector.tensor_copy(
                late[:, slot : slot + H], word_table[:, first : first + T].bitcast(U32).indirect(entries(EARLY, H))
            )
            multiply(o, D - 1, 1, late[:, slot : slot + H], o == PASSES - 1)

        results = keep.tile([P, T], F32, name="results")
        for h in range(2):
            positive = keep.tile([P, H], F32, name="positive%d" % h)
            if h == 0:
                nc.scalar.activation(positive[:], acc[h][:], ACT.Relu, bias=bias[:])
            else:
                nc.vector.tensor_scalar(positive[:], acc[h][:], bias[:], 0.0, mybir.AluOpType.add, mybir.AluOpType.max)
            slots = results[:].rearrange("p (d h v) -> p d h v", d=D, h=2)
            for d0, d1 in (((0, 1), (1, 4)) if h == 0 else ((0, 2), (2, 4))):
                nc.scalar.activation(
                    slots[:, d0:d1, h, :], positive[:].unsqueeze(1).to_broadcast([P, d1 - d0, H]), ACT.Square
                )

        placed = keep.tile([P, T], F32, name="placed")
        for first, count in ((0, H), (H, 4 * H), (5 * H, 3 * H)):
            nc.vector.tensor_tensor(
                placed[:].indirect(entries(first, count)),
                results[:, first : first + count],
                gates[:, first : first + count],
                MULT,
            )
        nc.sync.dma_start(out, placed[:])
